import numpy as np
import ml_dtypes


def mxq(x, axis, fmt="e4m3"):
    dtype, down = {"e4m3": (ml_dtypes.float8_e4m3fn, 7), "e5m2": (ml_dtypes.float8_e5m2, 14)}[fmt]
    v = np.moveaxis(np.asarray(x, np.float32).astype(ml_dtypes.bfloat16).astype(np.float64), axis, -1)
    blocks = v.reshape(v.shape[:-1] + (-1, 32))
    amax = np.abs(blocks).max(-1, keepdims=True)
    byte = np.maximum(np.where(amax > 0, np.frexp(amax)[1] - 1 + 127, 0) - down, 1)
    scale = np.exp2(byte - 127.0)
    codes = (blocks / scale).astype(np.float32).astype(dtype).astype(np.float64)
    return np.moveaxis((codes * scale).reshape(v.shape), -1, axis)


WIDE = False


def mx_kscale(k):
    if not WIDE:
        return np.ones(k)
    levels = np.array([10, -10, 5, -5, 0])
    if k % 512:
        return np.exp2(np.random.permutation(np.resize(levels, k // 32))).repeat(32)
    a = np.empty((k // 512, 16))
    for p in range(k // 512):
        a[p, :8] = np.random.permutation(np.resize(levels, 8))
        for g in range(8):
            far = levels[np.abs(levels - a[p, g]) >= 10]
            a[p, g + 8] = far[np.random.randint(len(far))]
    return np.exp2(a.ravel()).repeat(32)


BF16 = ml_dtypes.bfloat16


def bf(x):
    return np.asarray(x, np.float32).astype(BF16)


def f64(x):
    return np.asarray(x).astype(np.float64)

def planes(Y):
    n, m = Y.shape
    b = f64(bf(Y)).reshape(n // 32, 32, m)
    amax = np.abs(b).max(1)
    byte = np.clip(np.where(amax > 0, np.frexp(amax)[1] - 1 + 127 - 7, 1), 1, 254)
    codes = (b * np.exp2(127.0 - byte)[:, None, :]).reshape(n, m).astype(np.float32).astype(ml_dtypes.float8_e4m3fn).view(np.uint8)
    words = codes.reshape(n // 512, 128, 4, m).transpose(0, 1, 3, 2)
    return np.ascontiguousarray(words), np.ascontiguousarray(byte.astype(np.uint8).reshape(n // 512, 16, m))


C, S, P, Q = 1024, 1024, 1024, 1024


def weighted_influence(u, cutoff, weight):
    ratio = u / cutoff[None, :]
    return weight[:, None] * u / np.sqrt(1.0 + ratio * ratio)


def setup_inputs():
    s, t = mx_kscale(S), mx_kscale(C)
    return {
        "l": bf(np.random.standard_normal((C, S)) / np.sqrt(S) * s),
        "y": bf(np.random.standard_normal((S, P)) / s[:, None]),
        "z": bf(np.random.standard_normal((S, Q)) / s[:, None]),
        "cy": bf(np.random.uniform(0.7, 1.5, P)),
        "cz": bf(np.random.uniform(0.7, 1.5, Q)),
        "g1": bf((1.0 + 0.2 * np.random.standard_normal(C)) * t),
        "g2": bf((1.0 + 0.2 * np.random.standard_normal(C)) / t),
    }


def core(l, y, z, cy, cz, g1, g2):
    n_contrasts = l.shape[0]
    lq = mxq(f64(l), 1, "e4m3")
    u = lq @ mxq(f64(y), 0, "e4m3")
    v = lq @ mxq(f64(z), 0, "e4m3")
    a = weighted_influence(u, f64(cy), f64(g1))
    b = weighted_influence(v, f64(cz), f64(g2))
    aq = mxq(a, 0, "e4m3")
    bq = mxq(b, 0, "e4m3")
    return (aq.T @ bq) / np.sqrt(n_contrasts)


def reference(l, y, z, cy, cz, g1, g2):
    R_out = core(l, y, z, cy, cz, g1, g2)
    words, scales = planes(R_out)
    return R_out, words, scales

@@ -1,0 +1,413 @@
+from contextlib import ExitStack
+
+import concourse.mybir as mybir
+from concourse.masks import make_identity
+
+F32 = mybir.dt.float32
+BF16 = mybir.dt.bfloat16
+U32 = mybir.dt.uint32
+I32 = mybir.dt.int32
+U8 = mybir.dt.uint8
+FP8X4 = mybir.dt.float8_e4m3fn_x4
+ACTF = mybir.ActivationFunctionType
+ALU = mybir.AluOpType
+
+N = 1024
+P = 128
+FLOPS = 3 * 2 * N * N * N
+
+CHUNKS = ((0, 256), (256, 256), (512, 256), (768, 128), (896, 128))
+AHEAD = 3
+L_ENGINE = "act"
+Y1 = ("pool", "pool", "pool", "pool")
+Z0 = ("pool", "pool", "pool", "pool")
+Z1 = ("pool", "pool", "pool", "pool")
+OG = "pool"
+
+
+def tile_pseudohuberphylogeneticcontrastcrossmome_x1_kernel(
+    tc, l, y, z, cy, cz, g1, g2, out_0, out_1, out_2
+):
+    nc = tc.nc
+    with ExitStack() as ctx:
+        keep = ctx.enter_context(tc.tile_pool(name="keep", bufs=1))
+        work = ctx.enter_context(tc.tile_pool(name="work", bufs=3))
+        psum = ctx.enter_context(tc.psum_pool(name="psum", bufs=1))
+
+        def u_bank():
+            return psum.tile([P, 512], F32, name="u_ps", tag="u_ps", bufs=4)
+
+        def t_bank():
+            return psum.tile([P, 512], F32, name="t_ps", tag="to_ps", bufs=4)
+
+        def o_bank():
+            return psum.tile([P, 512], F32, name="o_ps", tag="to_ps", bufs=4)
+
+        rows = keep.tile([P, P], BF16, name="rows")
+        nc.vector.memset(rows[:], 0.0)
+        l_raw = [[keep.tile([P, 2, N], BF16, name="l_raw_%d_%d" % (g, tp)) for tp in range(2)] for g in range(2)]
+        l_view = l.rearrange("(g m t) s -> g m t s", g=2, t=4)
+
+        def load_l(g):
+            for tp in range(2):
+                nc.sync.dma_start(out=l_raw[g][tp][:], in_=l_view[g][:, 2 * tp : 2 * tp + 2, :])
+
+        raw = {}
+        views = {"y": y.rearrange("(h p j) w -> h p j w", h=2, j=4), "z": z.rearrange("(h p j) w -> h p j w", h=2, j=4)}
+
+        def load_yz(which, c):
+            for h in range(2):
+                tile = keep.tile([P, 4, 512], BF16, name="raw_%s_%d_%d" % (which, c, h))
+                nc.sync.dma_start(out=tile[:], in_=views[which][h][:, :, 512 * c : 512 * c + 512])
+                raw[which, c, h] = tile
+
+        load_l(0)
+        nc.scalar.dma_start(out=rows[0:8, :], in_=cy.rearrange("(i n) -> i n", n=P))
+        nc.scalar.dma_start(out=rows[8:16, :], in_=cz.rearrange("(i n) -> i n", n=P))
+        gain = []
+        for name, src in (("g1", g1), ("g2", g2)):
+            gt = keep.tile([P, 2, 4], BF16, name="gain_" + name)
+            nc.scalar.dma_start(out=gt[:], in_=src.rearrange("(g p t) -> p g t", g=2, t=4))
+            gain.append(gt)
+        load_yz("y", 0)
+        load_l(1)
+        load_yz("y", 1)
+        load_yz("z", 0)
+        load_yz("z", 1)
+
+        ident = keep.tile([P, P], F32, name="ident")
+        make_identity(nc, ident[:])
+
+        l_grp = [[keep.tile([P, 512, 4], BF16, name="l_grp_%d_%d" % (g, h), align_bytes=64) for h in range(2)] for g in range(2)]
+        l_codes = [[keep.tile([P, 512], U32, name="l_codes_%d_%d" % (g, h), align_bytes=64) for h in range(2)] for g in range(2)]
+        l_scales = [[keep.tile([P, 512], U8, name="l_scales_%d_%d" % (g, h), align_bytes=64) for h in range(2)] for g in range(2)]
+
+        def l_transpose(g, h, tp, bank):
+            words = l_raw[g][tp][:].rearrange("m t s -> m (t s)").bitcast(F32)
+            for u in range(2):
+                for tt in range(2):
+                    lo = 512 * tt + 256 * h
+                    nc.tensor.transpose(
+                        bank[:, 256 * u + 128 * tt : 256 * u + 128 * tt + 128], words[:, lo + u : lo + 256 : 2], ident[:]
+                    )
+
+        def l_copy(g, h, tp, bank, engine):
+            dst = l_grp[g][h][:, 256 * tp : 256 * tp + 256, :].rearrange("p r j -> p (r j)").bitcast(F32)
+            src = bank[:].rearrange("p (u r) -> p r u", u=2)
+            dst = dst.rearrange("p (r u) -> p r u", u=2)
+            if engine == "act":
+                nc.scalar.copy(out=dst, in_=src)
+            else:
+                nc.vector.tensor_copy(out=dst, in_=src)
+
+        def quantize(codes, scales, grp):
+            nc.vector.quantize_mx(out=codes.bitcast(FP8X4), scales=scales, in_=grp)
+
+        def l_quant(g, h):
+            quantize(l_codes[g][h][:], l_scales[g][h][:], l_grp[g][h][:].rearrange("p r j -> p (r j)"))
+
+        grp = {}
+        codes = {}
+        scales = {}
+
+        def interleave(key, lo, hi, engine):
+            if key not in grp:
+                grp[key] = keep.tile([P, 512, 4], BF16, name="grp_%s_%d_%d" % key, align_bytes=64)
+            dst = grp[key][:, lo:hi, :]
+            src = raw[key][:, :, lo:hi].rearrange("p j w -> p w j")
+            if engine == "act":
+                nc.scalar.copy(out=dst, in_=src)
+            elif engine == "pool":
+                nc.gpsimd.tensor_scalar(out=dst, in0=src, scalar1=1.0, scalar2=0.0, op0=ALU.mult, op1=ALU.add)
+            else:
+                nc.vector.tensor_copy(out=dst, in_=src)
+
+        def yz_quant(key, lo=0, hi=512):
+            if key not in codes:
+                codes[key] = keep.tile([P, 512], U32, name="codes_%s_%d_%d" % key, align_bytes=64)
+                scales[key] = keep.tile([P, 512], U8, name="scales_%s_%d_%d" % key, align_bytes=64)
+            quantize(codes[key][:, lo:hi], scales[key][:, lo:hi], grp[key][:, lo:hi, :].rearrange("p w j -> p (w j)"))
+
+        icut = keep.tile([P, 16], F32, name="icut")
+
+        units = []
+        for c in range(2):
+            for g in range(2):
+                for ii in range(4):
+                    units.append(("y", 4 * c + ii, g))
+        chunk_of = {}
+        for k, (lo, width) in enumerate(CHUNKS):
+            for g in range(2):
+                for tile in range(lo // 128, (lo + width) // 128):
+                    units.append(("z", tile, g))
+                    chunk_of[tile] = k
+
+        u_ps = {}
+        sq = {}
+        rs = {}
+        prod = {}
+        t_ps = {}
+
+        def mm(i):
+            which, tile, g = units[i]
+            u_ps[i] = u_bank()
+            c, lo = tile // 4, 128 * (tile % 4)
+            for h in range(2):
+                nc.tensor.matmul_mx(
+                    out=u_ps[i][:],
+                    lhsT=codes[which, c, h][:, lo : lo + 128].bitcast(FP8X4),
+                    lhsT_scale=scales[which, c, h][:, lo : lo + 128],
+                    rhs=l_codes[g][h][:].bitcast(FP8X4),
+                    rhs_scale=l_scales[g][h][:],
+                    start=(h == 0),
+                    stop=(h == 1),
+                )
+
+        def square(i):
+            which, tile, g = units[i]
+            col = tile + (8 if which == "z" else 0)
+            sq[i] = work.tile([P, 512], F32, name="sq", bufs=4)
+            nc.scalar.activation(out=sq[i][:], in_=u_ps[i][:], func=ACTF.Square, scale=icut[:, col : col + 1])
+
+        def rsqrt(i):
+            rs[i] = work.tile([P, 512], F32, name="rs", bufs=4)
+            nc.scalar.activation(out=rs[i][:], in_=sq[i][:], func=ACTF.Abs_reciprocal_sqrt, bias=1.0, scale=1.0)
+
+        def product(i):
+            prod[i] = work.tile([P, 512], F32, name="prod", bufs=3)
+            nc.vector.tensor_tensor(out=prod[i][:], in0=u_ps[i][:], in1=rs[i][:], op=ALU.mult)
+
+        def turn(i):
+            t_ps[i] = t_bank()
+            for t in range(4):
+                nc.tensor.transpose(t_ps[i][:, 128 * t : 128 * t + 128], prod[i][:, 128 * t : 128 * t + 128], ident[:])
+
+        ab_grp = {}
+        ab_codes = {}
+        ab_scales = {}
+        for which in "yz":
+            for g in range(2):
+                ab_codes[which, g] = keep.tile([P, N], U32, name="ab_codes_%s_%d" % (which, g), align_bytes=64)
+                ab_scales[which, g] = keep.tile([P, N], U8, name="ab_scales_%s_%d" % (which, g), align_bytes=64)
+
+        def weigh(i):
+            which, tile, g = units[i]
+            if which == "y":
+                c, ii = tile // 4, tile % 4
+                key = (which, c, g)
+                if key not in ab_grp:
+                    ab_grp[key] = work.tile([P, 512, 4], BF16, name="a_grp", bufs=2, align_bytes=64)
+                dst = ab_grp[key][:].rearrange("p (t m) j -> p t m j", t=4)[:, :, 32 * ii : 32 * ii + 32, :]
+                src = t_ps[i][:].rearrange("k (j m t) -> k t m j", j=4, t=4)
+                fac = gain[0][:, g, :].unsqueeze(1).unsqueeze(1).to_broadcast([P, 4, 32, 4])
+            else:
+                k = chunk_of[tile]
+                ii = tile - CHUNKS[k][0] // 128
+                key = (which, k, g)
+                if key not in ab_grp:
+                    ab_grp[key] = work.tile([P, 256, 4], BF16, name="b_grp", bufs=3, align_bytes=64)
+                dst = ab_grp[key][:, 128 * ii : 128 * ii + 128, :]
+                src = t_ps[i][:].rearrange("k (j n) -> k n j", j=4)
+                fac = gain[1][:, g, :].unsqueeze(1).to_broadcast([P, 128, 4])
+            nc.vector.tensor_tensor(out=dst, in0=src, in1=fac, op=ALU.mult)
+
+        def ab_quant(key):
+            which, c, g = key
+            lo, width = (512 * c, 512) if which == "y" else CHUNKS[c]
+            cols = slice(lo, lo + width)
+            quantize(
+                ab_codes[which, g][:, cols], ab_scales[which, g][:, cols], ab_grp[key][:, 0:width, :].rearrange("p w j -> p (w j)")
+            )
+
+        o_ps = {}
+        of = {}
+        og = {}
+        w_codes = {}
+        w_scales = {}
+
+        def out_mm(job):
+            k, big, first, count = job
+            lo, width = CHUNKS[k]
+            o_ps[job] = o_bank()
+            for tt in range(count):
+                row = 512 * big + 128 * (first + tt)
+                for g in range(2):
+                    nc.tensor.matmul_mx(
+                        out=o_ps[job][:, width * tt : width * tt + width],
+                        lhsT=ab_codes["y", g][:, row : row + 128].bitcast(FP8X4),
+                        lhsT_scale=ab_scales["y", g][:, row : row + 128],
+                        rhs=ab_codes["z", g][:, lo : lo + width].bitcast(FP8X4),
+                        rhs_scale=ab_scales["z", g][:, lo : lo + width],
+                        start=(g == 0),
+                        stop=(g == 1),
+                    )
+
+        def out_copy(job, engine):
+            k, big, first, count = job
+            lo, width = CHUNKS[k]
+            if first == 0:
+                of[k, big] = work.tile([P, 4, 256], F32, name="of", bufs=6)
+            dst = of[k, big][:, first : first + count, 0:width]
+            src = o_ps[job][:].rearrange("p (t m) -> p t m", t=count)
+            if engine == "act":
+                nc.scalar.activation(out=dst, in_=src, func=ACTF.Copy, scale=1.0 / 32.0)
+            else:
+                nc.vector.tensor_scalar(out=dst, in0=src, scalar1=1.0 / 32.0, scalar2=None, op0=ALU.mult)
+            if first + count == 4:
+                nc.sync.dma_start(
+                    out=out_0[512 * big : 512 * big + 512, lo : lo + width].rearrange("(p t) m -> p t m", t=4),
+                    in_=of[k, big][:, :, 0:width],
+                )
+
+        def out_group(k, big, engine):
+            width = CHUNKS[k][1]
+            og[k, big] = work.tile([P, 256, 4], BF16, name="og", bufs=4, align_bytes=64)
+            dst = og[k, big][:, 0:width, :]
+            src = of[k, big][:, :, 0:width].rearrange("p t m -> p m t")
+            if engine == "pool":
+                nc.gpsimd.tensor_scalar(out=dst, in0=src, scalar1=1.0, scalar2=0.0, op0=ALU.mult, op1=ALU.add)
+            else:
+                nc.vector.tensor_copy(out=dst, in_=src)
+
+        def out_quant(k, big):
+            lo, width = CHUNKS[k]
+            if big == 0:
+                w_scales[k] = work.tile([P, 2, 256], U8, name="w_scales", bufs=4, align_bytes=64)
+            wc = work.tile([P, 256], U32, name="w_codes", bufs=6, align_bytes=64)
+            quantize(wc[:, 0:width], w_scales[k][:, big, 0:width], og[k, big][:, 0:width, :].rearrange("p m t -> p (m t)"))
+            nc.sync.dma_start(
+                out=out_1[big][:, lo : lo + width, :].rearrange("p m t -> p (m t)").bitcast(I32), in_=wc[:, 0:width].bitcast(I32)
+            )
+            if big == 1:
+                for q in range(4):
+                    nc.sync.dma_start(
+                        out=out_2[:, 4 * q : 4 * q + 4, lo : lo + width].rearrange("g r m -> r g m").bitcast(I32),
+                        in_=w_scales[k][32 * q : 32 * q + 4, :, 0:width].bitcast(I32),
+                    )
+
+        with tc.manual_schedule(engines={mybir.EngineType.PE, mybir.EngineType.Activation, mybir.EngineType.DVE}):
+            warm = keep.tile([P, 1], F32, name="warm")
+            nc.vector.memset(warm[:], 1.0)
+            nc.scalar.activation(out=warm[:], in_=warm[:], func=ACTF.Abs_reciprocal_sqrt, bias=1.0, scale=1.0)
+
+            rows32 = keep.tile([P, P], F32, name="rows32")
+            nc.vector.tensor_copy(out=rows32[:], in_=rows[:])
+            cut_ps = t_bank()
+            nc.tensor.transpose(cut_ps[:, 0:128], rows32[:], ident[:])
+            nc.vector.reciprocal(out=icut[:], in_=cut_ps[:, 0:16])
+            for tp in range(2):
+                banks = [u_bank(), u_bank()]
+                for h in range(2):
+                    l_transpose(0, h, tp, banks[h])
+                l_copy(0, 0, tp, banks[0], "act")
+                l_copy(0, 1, tp, banks[1], "dve" if tp == 0 else "act")
+            l_quant(0, 0)
+            l_quant(0, 1)
+            interleave(("y", 0, 0), 0, 256, "act")
+            interleave(("y", 0, 1), 0, 256, "dve")
+            yz_quant(("y", 0, 0), 0, 256)
+            yz_quant(("y", 0, 1), 0, 256)
+
+            side = {}
+
+            def add_side(step, job):
+                side.setdefault(step, []).append(job)
+
+            l_banks = {}
+
+            def l_turn(tp):
+                for h in range(2):
+                    l_banks[tp, h] = o_bank()
+                    l_transpose(1, h, tp, l_banks[tp, h])
+
+            def l_out(tp):
+                l_copy(1, 0, tp, l_banks[tp, 0], "act")
+                l_copy(1, 1, tp, l_banks[tp, 1], L_ENGINE)
+
+            def half(key, lo, engine):
+                return lambda: interleave(key, lo, lo + 256, engine)
+
+            def quant_job(key):
+                return lambda: yz_quant(key)
+
+            add_side(0, lambda: l_quant(1, 0))
+            add_side(0, lambda: l_quant(1, 1))
+            for n in range(4):
+                add_side(1, half(("y", 1, n // 2), 256 * (n % 2), Y1[n]))
+            add_side(3, quant_job(("y", 1, 0)))
+            add_side(4, quant_job(("y", 1, 1)))
+            for n in range(4):
+                add_side(5, half(("z", 0, n // 2), 256 * (n % 2), Z0[n]))
+            add_side(10, quant_job(("z", 0, 0)))
+            add_side(11, quant_job(("z", 0, 1)))
+            for n in range(4):
+                add_side(12, half(("z", 1, n // 2), 256 * (n % 2), Z1[n]))
+            add_side(17, quant_job(("z", 1, 0)))
+            add_side(18, quant_job(("z", 1, 1)))
+
+            last_of = {}
+            for i, (which, tile, g) in enumerate(units):
+                last_of[which, tile // 4 if which == "y" else chunk_of[tile], g] = i
+            key_after = {i: key for key, i in last_of.items()}
+
+            jobs = []
+            copies = []
+            groups = []
+            quants = []
+            n = len(units)
+            mm(0)
+            mm(1)
+            interleave(("y", 0, 0), 256, 512, "act")
+            interleave(("y", 0, 1), 256, 512, "pool")
+            yz_quant(("y", 0, 0), 256, 512)
+            yz_quant(("y", 0, 1), 256, 512)
+            square(0)
+            l_turn(0)
+            mm(2)
+            square(1)
+            rsqrt(0)
+            l_turn(1)
+            l_out(0)
+            l_out(1)
+            i = 0
+            done = 0
+            while i < n + 2 or jobs or copies or groups or quants:
+                if i + AHEAD < n:
+                    mm(i + AHEAD)
+                new_copy = []
+                for unused in range(1 if i < n + 1 else 2):
+                    if jobs:
+                        job = jobs.pop(0)
+                        out_mm(job)
+                        new_copy.append(job)
+                if i + 2 < n:
+                    square(i + 2)
+                if i + 1 < n:
+                    rsqrt(i + 1)
+                if i < n:
+                    product(i)
+                    turn(i)
+                if 1 <= i <= n:
+                    weigh(i - 1)
+                if quants:
+                    out_quant(*quants.pop(0))
+                if groups:
+                    grp_key = groups.pop(0)
+                    out_group(grp_key[0], grp_key[1], OG if i < n else "dve")
+                    quants.append(grp_key)
+                for m, job in enumerate(copies):
+                    out_copy(job, "act" if m == 0 else "dve")
+                    if job[2] + job[3] == 4:
+                        groups.append((job[0], job[1]))
+                copies = new_copy
+                for job in side.get(i, []):
+                    job()
+                while done < (i - 1 if i < n else n):
+                    key = key_after.get(done)
+                    done += 1
+                    if key is not None:
+                        ab_quant(key)
+                        if key[0] == "z" and key[2] == 1:
+                            count = 512 // CHUNKS[key[1]][1]
+                            jobs.extend((key[1], big, first, count) for big in range(2) for first in range(0, 4, count))
+                i += 1

@@ -18,11 +18,19 @@ FLOPS = 3 * 2 * N * N * N
 
 CHUNKS = ((0, 256), (256, 256), (512, 256), (768, 128), (896, 128))
 AHEAD = 3
-L_ENGINE = "act"
-Y1 = ("pool", "pool", "pool", "pool")
-Z0 = ("pool", "pool", "pool", "pool")
-Z1 = ("pool", "pool", "pool", "pool")
-OG = "pool"
+LAG = 1
+UB = 4
+L0 = ('act', 'dve', 'dve', 'dve')
+L1 = ('act', 'act', 'dve', 'act')
+Y0 = ('act', 'act', 'act', 'dve')
+Y1 = ('act', 'pool', 'pool', 'pool')
+Z0 = ('pool', 'pool', 'pool', 'act')
+Z1 = ('pool', 'act', 'pool', 'pool')
+OG = ('dve', 'dve', 'pool', 'act', 'act', 'dve', 'dve', 'act', 'act', 'dve')
+OUT = ('act', 'dve', 'act', 'act', 'dve', 'act', 'act', 'act', 'act', 'act', 'act', 'dve', 'dve', 'act', 'act', 'dve', 'act', 'dve')
+YSTEP, Z0STEP, Z1STEP = (0, 2, 16)
+YQ, Z0Q, Z1Q = ((1, 3), (12, 9), (18, 16))
+PIECE = 128
 
 
 def tile_pseudohuberphylogeneticcontrastcrossmome_x1_kernel(
@@ -35,31 +43,43 @@ def tile_pseudohuberphylogeneticcontrastcrossmome_x1_kernel(
         psum = ctx.enter_context(tc.psum_pool(name="psum", bufs=1))
 
         def u_bank():
-            return psum.tile([P, 512], F32, name="u_ps", tag="u_ps", bufs=4)
+            return psum.tile([P, 512], F32, name="u_ps", tag="u_ps", bufs=UB)
 
         def t_bank():
-            return psum.tile([P, 512], F32, name="t_ps", tag="to_ps", bufs=4)
+            return psum.tile([P, 512], F32, name="t_ps", tag="to_ps", bufs=8 - UB)
 
         def o_bank():
-            return psum.tile([P, 512], F32, name="o_ps", tag="to_ps", bufs=4)
+            return psum.tile([P, 512], F32, name="o_ps", tag="to_ps", bufs=8 - UB)
 
         rows = keep.tile([P, P], BF16, name="rows")
         nc.vector.memset(rows[:], 0.0)
-        l_raw = [[keep.tile([P, 2, N], BF16, name="l_raw_%d_%d" % (g, tp)) for tp in range(2)] for g in range(2)]
+        l_raw = {}
         l_view = l.rearrange("(g m t) s -> g m t s", g=2, t=4)
 
         def load_l(g):
-            for tp in range(2):
-                nc.sync.dma_start(out=l_raw[g][tp][:], in_=l_view[g][:, 2 * tp : 2 * tp + 2, :])
+            if g == 0:
+                for t in range(4):
+                    tile = keep.tile([P, N], BF16, name="l_raw_0_%d" % t)
+                    nc.sync.dma_start(out=tile[:], in_=l_view[g][:, t, :])
+                    l_raw[g, t] = tile[:]
+            else:
+                for tp in range(2):
+                    tile = keep.tile([P, 2, N], BF16, name="l_raw_1_%d" % tp)
+                    nc.sync.dma_start(out=tile[:], in_=l_view[g][:, 2 * tp : 2 * tp + 2, :])
+                    l_raw[g, 2 * tp] = tile[:, 0, :]
+                    l_raw[g, 2 * tp + 1] = tile[:, 1, :]
 
         raw = {}
         views = {"y": y.rearrange("(h p j) w -> h p j w", h=2, j=4), "z": z.rearrange("(h p j) w -> h p j w", h=2, j=4)}
 
         def load_yz(which, c):
-            for h in range(2):
-                tile = keep.tile([P, 4, 512], BF16, name="raw_%s_%d_%d" % (which, c, h))
-                nc.sync.dma_start(out=tile[:], in_=views[which][h][:, :, 512 * c : 512 * c + 512])
-                raw[which, c, h] = tile
+            width = 256 if (which, c) == ("y", 0) else 512
+            for lo in range(0, 512, width):
+                for h in range(2):
+                    tile = keep.tile([P, 4, width], BF16, name="raw_%s_%d_%d_%d" % (which, c, h, lo))
+                    nc.sync.dma_start(out=tile[:], in_=views[which][h][:, :, 512 * c + lo : 512 * c + lo + width])
+                    for at in range(lo, lo + width, 128):
+                        raw[which, c, h, at] = (tile, at - lo)
 
         load_l(0)
         nc.scalar.dma_start(out=rows[0:8, :], in_=cy.rearrange("(i n) -> i n", n=P))
@@ -82,13 +102,14 @@ def tile_pseudohuberphylogeneticcontrastcrossmome_x1_kernel(
         l_codes = [[keep.tile([P, 512], U32, name="l_codes_%d_%d" % (g, h), align_bytes=64) for h in range(2)] for g in range(2)]
         l_scales = [[keep.tile([P, 512], U8, name="l_scales_%d_%d" % (g, h), align_bytes=64) for h in range(2)] for g in range(2)]
 
-        def l_transpose(g, h, tp, bank):
-            words = l_raw[g][tp][:].rearrange("m t s -> m (t s)").bitcast(F32)
-            for u in range(2):
-                for tt in range(2):
-                    lo = 512 * tt + 256 * h
+        def l_transpose(g, h, tp, bank, slots=(0, 1)):
+            for tt in slots:
+                words = l_raw[g, 2 * tp + tt].bitcast(F32)
+                for u in range(2):
                     nc.tensor.transpose(
-                        bank[:, 256 * u + 128 * tt : 256 * u + 128 * tt + 128], words[:, lo + u : lo + 256 : 2], ident[:]
+                        bank[:, 256 * u + 128 * tt : 256 * u + 128 * tt + 128],
+                        words[:, 256 * h + u : 256 * h + 256 : 2],
+                        ident[:],
                     )
 
         def l_copy(g, h, tp, bank, engine):
@@ -103,8 +124,8 @@ def tile_pseudohuberphylogeneticcontrastcrossmome_x1_kernel(
         def quantize(codes, scales, grp):
             nc.vector.quantize_mx(out=codes.bitcast(FP8X4), scales=scales, in_=grp)
 
-        def l_quant(g, h):
-            quantize(l_codes[g][h][:], l_scales[g][h][:], l_grp[g][h][:].rearrange("p r j -> p (r j)"))
+        def l_quant(g, h, lo=0, hi=512):
+            quantize(l_codes[g][h][:, lo:hi], l_scales[g][h][:, lo:hi], l_grp[g][h][:, lo:hi, :].rearrange("p r j -> p (r j)"))
 
         grp = {}
         codes = {}
@@ -114,7 +135,8 @@ def tile_pseudohuberphylogeneticcontrastcrossmome_x1_kernel(
             if key not in grp:
                 grp[key] = keep.tile([P, 512, 4], BF16, name="grp_%s_%d_%d" % key, align_bytes=64)
             dst = grp[key][:, lo:hi, :]
-            src = raw[key][:, :, lo:hi].rearrange("p j w -> p w j")
+            tile, at = raw[key[0], key[1], key[2], lo]
+            src = tile[:, :, at : at + hi - lo].rearrange("p j w -> p w j")
             if engine == "act":
                 nc.scalar.copy(out=dst, in_=src)
             elif engine == "pool":
@@ -266,6 +288,8 @@ def tile_pseudohuberphylogeneticcontrastcrossmome_x1_kernel(
             src = of[k, big][:, :, 0:width].rearrange("p t m -> p m t")
             if engine == "pool":
                 nc.gpsimd.tensor_scalar(out=dst, in0=src, scalar1=1.0, scalar2=0.0, op0=ALU.mult, op1=ALU.add)
+            elif engine == "act":
+                nc.scalar.copy(out=dst, in_=src)
             else:
                 nc.vector.tensor_copy(out=dst, in_=src)
 
@@ -290,21 +314,23 @@ def tile_pseudohuberphylogeneticcontrastcrossmome_x1_kernel(
             nc.vector.memset(warm[:], 1.0)
             nc.scalar.activation(out=warm[:], in_=warm[:], func=ACTF.Abs_reciprocal_sqrt, bias=1.0, scale=1.0)
 
-            rows32 = keep.tile([P, P], F32, name="rows32")
-            nc.vector.tensor_copy(out=rows32[:], in_=rows[:])
+            for tp in range(2):
+                banks = [u_bank(), u_bank()]
+                for tt in range(2):
+                    for h in range(2):
+                        l_transpose(0, h, tp, banks[h], (tt,))
+                for h in range(2):
+                    l_copy(0, h, tp, banks[h], L0[2 * tp + h])
+                if tp == 0:
+                    rows32 = keep.tile([P, P], F32, name="rows32")
+                    nc.vector.tensor_copy(out=rows32[:], in_=rows[:])
+                for h in range(2):
+                    l_quant(0, h, 256 * tp, 256 * tp + 256)
             cut_ps = t_bank()
             nc.tensor.transpose(cut_ps[:, 0:128], rows32[:], ident[:])
             nc.vector.reciprocal(out=icut[:], in_=cut_ps[:, 0:16])
-            for tp in range(2):
-                banks = [u_bank(), u_bank()]
-                for h in range(2):
-                    l_transpose(0, h, tp, banks[h])
-                l_copy(0, 0, tp, banks[0], "act")
-                l_copy(0, 1, tp, banks[1], "dve" if tp == 0 else "act")
-            l_quant(0, 0)
-            l_quant(0, 1)
-            interleave(("y", 0, 0), 0, 256, "act")
-            interleave(("y", 0, 1), 0, 256, "dve")
+            interleave(("y", 0, 0), 0, 256, Y0[0])
+            interleave(("y", 0, 1), 0, 256, Y0[1])
             yz_quant(("y", 0, 0), 0, 256)
             yz_quant(("y", 0, 1), 0, 256)
 
@@ -321,29 +347,27 @@ def tile_pseudohuberphylogeneticcontrastcrossmome_x1_kernel(
                     l_transpose(1, h, tp, l_banks[tp, h])
 
             def l_out(tp):
-                l_copy(1, 0, tp, l_banks[tp, 0], "act")
-                l_copy(1, 1, tp, l_banks[tp, 1], L_ENGINE)
+                l_copy(1, 0, tp, l_banks[tp, 0], L1[2 * tp])
+                l_copy(1, 1, tp, l_banks[tp, 1], L1[2 * tp + 1])
 
             def half(key, lo, engine):
-                return lambda: interleave(key, lo, lo + 256, engine)
+                def run():
+                    piece = PIECE if engine == "pool" else 256
+                    for at in range(lo, lo + 256, piece):
+                        interleave(key, at, at + piece, engine)
+
+                return run
 
             def quant_job(key):
                 return lambda: yz_quant(key)
 
             add_side(0, lambda: l_quant(1, 0))
             add_side(0, lambda: l_quant(1, 1))
-            for n in range(4):
-                add_side(1, half(("y", 1, n // 2), 256 * (n % 2), Y1[n]))
-            add_side(3, quant_job(("y", 1, 0)))
-            add_side(4, quant_job(("y", 1, 1)))
-            for n in range(4):
-                add_side(5, half(("z", 0, n // 2), 256 * (n % 2), Z0[n]))
-            add_side(10, quant_job(("z", 0, 0)))
-            add_side(11, quant_job(("z", 0, 1)))
-            for n in range(4):
-                add_side(12, half(("z", 1, n // 2), 256 * (n % 2), Z1[n]))
-            add_side(17, quant_job(("z", 1, 0)))
-            add_side(18, quant_job(("z", 1, 1)))
+            for which, c, plan, first, at in (("y", 1, Y1, YSTEP, YQ), ("z", 0, Z0, Z0STEP, Z0Q), ("z", 1, Z1, Z1STEP, Z1Q)):
+                for m in range(4):
+                    add_side(first + (m if plan[m] != "pool" else 0), half((which, c, m // 2), 256 * (m % 2), plan[m]))
+                for h in range(2):
+                    add_side(at[h], quant_job((which, c, h)))
 
             last_of = {}
             for i, (which, tile, g) in enumerate(units):
@@ -357,8 +381,8 @@ def tile_pseudohuberphylogeneticcontrastcrossmome_x1_kernel(
             n = len(units)
             mm(0)
             mm(1)
-            interleave(("y", 0, 0), 256, 512, "act")
-            interleave(("y", 0, 1), 256, 512, "pool")
+            interleave(("y", 0, 0), 256, 512, Y0[2])
+            interleave(("y", 0, 1), 256, 512, Y0[3])
             yz_quant(("y", 0, 0), 256, 512)
             yz_quant(("y", 0, 1), 256, 512)
             square(0)
@@ -371,11 +395,12 @@ def tile_pseudohuberphylogeneticcontrastcrossmome_x1_kernel(
             l_out(1)
             i = 0
             done = 0
-            while i < n + 2 or jobs or copies or groups or quants:
+            copied = 0
+            while i < n + LAG or jobs or copies or groups or quants:
                 if i + AHEAD < n:
                     mm(i + AHEAD)
                 new_copy = []
-                for unused in range(1 if i < n + 1 else 2):
+                for unused in range(1 if i < n + LAG else 2):
                     if jobs:
                         job = jobs.pop(0)
                         out_mm(job)
@@ -387,22 +412,23 @@ def tile_pseudohuberphylogeneticcontrastcrossmome_x1_kernel(
                 if i < n:
                     product(i)
                     turn(i)
-                if 1 <= i <= n:
-                    weigh(i - 1)
-                if quants:
-                    out_quant(*quants.pop(0))
+                if LAG <= i < n + LAG:
+                    weigh(i - LAG)
                 if groups:
                     grp_key = groups.pop(0)
-                    out_group(grp_key[0], grp_key[1], OG if i < n else "dve")
+                    out_group(grp_key[0], grp_key[1], OG[2 * grp_key[0] + grp_key[1]])
                     quants.append(grp_key)
+                if len(quants) > (1 if groups or copies or i < n else 0):
+                    out_quant(*quants.pop(0))
                 for m, job in enumerate(copies):
-                    out_copy(job, "act" if m == 0 else "dve")
+                    out_copy(job, OUT[copied])
+                    copied += 1
                     if job[2] + job[3] == 4:
                         groups.append((job[0], job[1]))
                 copies = new_copy
                 for job in side.get(i, []):
                     job()
-                while done < (i - 1 if i < n else n):
+                while done < (i - LAG if i < n else i - LAG + 1):
                     key = key_after.get(done)
                     done += 1
                     if key is not None:

@@ -16,21 +16,19 @@ N = 1024
 P = 128
 FLOPS = 3 * 2 * N * N * N
 
-CHUNKS = ((0, 256), (256, 256), (512, 256), (768, 128), (896, 128))
-AHEAD = 3
-LAG = 1
-UB = 4
-L0 = ('act', 'dve', 'dve', 'dve')
-L1 = ('act', 'act', 'dve', 'act')
-Y0 = ('act', 'act', 'act', 'dve')
-Y1 = ('act', 'pool', 'pool', 'pool')
-Z0 = ('pool', 'pool', 'pool', 'act')
-Z1 = ('pool', 'act', 'pool', 'pool')
-OG = ('dve', 'dve', 'pool', 'act', 'act', 'dve', 'dve', 'act', 'act', 'dve')
-OUT = ('act', 'dve', 'act', 'act', 'dve', 'act', 'act', 'act', 'act', 'act', 'act', 'dve', 'dve', 'act', 'act', 'dve', 'act', 'dve')
-YSTEP, Z0STEP, Z1STEP = (0, 2, 16)
-YQ, Z0Q, Z1Q = ((1, 3), (12, 9), (18, 16))
+CHUNKS = ((0, 256), (256, 256), (512, 256), (768, 256))
 PIECE = 128
+LAG = 1
+UORD = 'cg'
+UB = 4
+MA = 3
+TAILJ = 2
+EARLYJ = 1
+QLAG = 1
+L0 = ('dve', 'act', 'act', 'dve')
+OG = ('pool', 'pool', 'pool', 'pool', 'act', 'dve', 'dve', 'dve', 'dve', 'dve', 'dve', 'dve')
+OUT = ('act',) * 11 + ('dve',) + ('act',) * 2 + ('dve',) + ('act',) * 5
+SIDE = ((-4, 'copy', 'y', 0, 0, 0, 'act'), (-4, 'copy', 'y', 0, 1, 0, 'act'), (-4, 'copy', 'y', 0, 1, 256, 'pool'), (-4, 'quant', 'y', 0, 0, 0, 256), (-4, 'quant', 'y', 0, 1, 0, 256), (-4, 'turn', 0), (-3, 'copy', 'y', 0, 0, 256, 'act'), (-3, 'quant', 'y', 0, 1, 256, 512), (-3, 'copy', 'y', 1, 0, 0, 'pool'), (-2, 'quant', 'y', 0, 0, 256, 512), (-2, 'turn', 1), (-2, 'copy', 'y', 1, 0, 256, 'pool'), (-2, 'lout', 0, 0, 'dve'), (-1, 'lout', 1, 0, 'dve'), (-1, 'lout', 1, 1, 'dve'), (-1, 'lout', 0, 1, 'act'), (-1, 'lquant', 0), (-1, 'copy', 'y', 1, 1, 0, 'pool'), (0, 'lquant', 1), (1, 'copy', 'y', 1, 1, 256, 'pool'), (2, 'copy', 'z', 0, 0, 0, 'pool'), (2, 'quant', 'y', 1, 0, 0, 512), (4, 'quant', 'y', 1, 1, 0, 512), (5, 'copy', 'z', 0, 0, 256, 'pool'), (7, 'copy', 'z', 0, 1, 0, 'pool'), (7, 'quant', 'z', 0, 0, 0, 512), (8, 'copy', 'z', 0, 1, 256, 'pool'), (9, 'copy', 'z', 1, 0, 0, 'pool'), (9, 'copy', 'z', 1, 0, 256, 'act'), (10, 'quant', 'z', 0, 1, 0, 512), (12, 'quant', 'z', 1, 0, 0, 512), (13, 'copy', 'z', 1, 1, 0, 'pool'), (14, 'copy', 'z', 1, 1, 256, 'act'), (15, 'quant', 'z', 1, 1, 0, 512))
 
 
 def tile_pseudohuberphylogeneticcontrastcrossmome_x1_kernel(
@@ -90,8 +88,12 @@ def tile_pseudohuberphylogeneticcontrastcrossmome_x1_kernel(
             nc.scalar.dma_start(out=gt[:], in_=src.rearrange("(g p t) -> p g t", g=2, t=4))
             gain.append(gt)
         load_yz("y", 0)
-        load_l(1)
-        load_yz("y", 1)
+        if UORD == "gc":
+            load_yz("y", 1)
+            load_l(1)
+        else:
+            load_l(1)
+            load_yz("y", 1)
         load_yz("z", 0)
         load_yz("z", 1)
 
@@ -136,7 +138,12 @@ def tile_pseudohuberphylogeneticcontrastcrossmome_x1_kernel(
                 grp[key] = keep.tile([P, 512, 4], BF16, name="grp_%s_%d_%d" % key, align_bytes=64)
             dst = grp[key][:, lo:hi, :]
             tile, at = raw[key[0], key[1], key[2], lo]
-            src = tile[:, :, at : at + hi - lo].rearrange("p j w -> p w j")
+            src = tile[:, :, at : at + hi - lo]
+            if engine == "pool":
+                src = src.rearrange("p j w -> p w j")
+            else:
+                src = src.rearrange("p j (w i) -> p w j i", i=4)
+                dst = dst.rearrange("p (w i) j -> p w j i", i=4)
             if engine == "act":
                 nc.scalar.copy(out=dst, in_=src)
             elif engine == "pool":
@@ -153,8 +160,9 @@ def tile_pseudohuberphylogeneticcontrastcrossmome_x1_kernel(
         icut = keep.tile([P, 16], F32, name="icut")
 
         units = []
-        for c in range(2):
-            for g in range(2):
+        for first in range(2):
+            for second in range(2):
+                c, g = (first, second) if UORD == "cg" else (second, first)
                 for ii in range(4):
                     units.append(("y", 4 * c + ii, g))
         chunk_of = {}
@@ -245,7 +253,6 @@ def tile_pseudohuberphylogeneticcontrastcrossmome_x1_kernel(
         of = {}
         og = {}
         w_codes = {}
-        w_scales = {}
 
         def out_mm(job):
             k, big, first, count = job
@@ -285,7 +292,21 @@ def tile_pseudohuberphylogeneticcontrastcrossmome_x1_kernel(
             width = CHUNKS[k][1]
             og[k, big] = work.tile([P, 256, 4], BF16, name="og", bufs=4, align_bytes=64)
             dst = og[k, big][:, 0:width, :]
-            src = of[k, big][:, :, 0:width].rearrange("p t m -> p m t")
+            if engine == "psum":
+                src = o_ps[k, big, 0, 4][:].rearrange("p (t m) -> p m t", t=4)
+                nc.vector.tensor_scalar(out=dst, in0=src, scalar1=1.0 / 32.0, scalar2=None, op0=ALU.mult)
+                return
+            src = of[k, big][:, :, 0:width]
+            if engine == "pool":
+                src = src.rearrange("p t m -> p m t")
+                for lo in range(0, width, PIECE):
+                    nc.gpsimd.tensor_scalar(
+                        out=dst[:, lo : lo + PIECE, :], in0=src[:, lo : lo + PIECE, :], scalar1=1.0, scalar2=0.0, op0=ALU.mult, op1=ALU.add
+                    )
+                return
+            else:
+                src = src.rearrange("p t (m i) -> p m t i", i=4)
+                dst = dst.rearrange("p (m i) t -> p m t i", i=4)
             if engine == "pool":
                 nc.gpsimd.tensor_scalar(out=dst, in0=src, scalar1=1.0, scalar2=0.0, op0=ALU.mult, op1=ALU.add)
             elif engine == "act":
@@ -293,21 +314,30 @@ def tile_pseudohuberphylogeneticcontrastcrossmome_x1_kernel(
             else:
                 nc.vector.tensor_copy(out=dst, in_=src)
 
+        w_scales = [keep.tile([P, 2, 512], U8, name="w_scales_%d" % half, align_bytes=64) for half in range(2)]
+
         def out_quant(k, big):
             lo, width = CHUNKS[k]
             if big == 0:
-                w_scales[k] = work.tile([P, 2, 256], U8, name="w_scales", bufs=4, align_bytes=64)
-            wc = work.tile([P, 256], U32, name="w_codes", bufs=6, align_bytes=64)
-            quantize(wc[:, 0:width], w_scales[k][:, big, 0:width], og[k, big][:, 0:width, :].rearrange("p m t -> p (m t)"))
-            nc.sync.dma_start(
-                out=out_1[big][:, lo : lo + width, :].rearrange("p m t -> p (m t)").bitcast(I32), in_=wc[:, 0:width].bitcast(I32)
+                w_codes[k] = work.tile([P, 2, 256], U32, name="w_codes", bufs=4, align_bytes=64)
+            plane = w_scales[lo // 512]
+            quantize(
+                w_codes[k][:, big, 0:width],
+                plane[:, big, lo % 512 : lo % 512 + width],
+                og[k, big][:, 0:width, :].rearrange("p m t -> p (m t)"),
             )
             if big == 1:
-                for q in range(4):
-                    nc.sync.dma_start(
-                        out=out_2[:, 4 * q : 4 * q + 4, lo : lo + width].rearrange("g r m -> r g m").bitcast(I32),
-                        in_=w_scales[k][32 * q : 32 * q + 4, :, 0:width].bitcast(I32),
-                    )
+                nc.sync.dma_start(
+                    out=out_1[:, :, lo : lo + width, :].rearrange("g p m t -> p g (m t)").bitcast(I32),
+                    in_=w_codes[k][:, :, 0:width].bitcast(I32),
+                )
+                if (lo + width) % 512 == 0:
+                    half = lo // 512
+                    for q in range(4):
+                        nc.sync.dma_start(
+                            out=out_2[:, 4 * q : 4 * q + 4, 512 * half : 512 * half + 512].rearrange("g r m -> r g m").bitcast(I32),
+                            in_=plane[32 * q : 32 * q + 4, :, :].bitcast(I32),
+                        )
 
         with tc.manual_schedule(engines={mybir.EngineType.PE, mybir.EngineType.Activation, mybir.EngineType.DVE}):
             warm = keep.tile([P, 1], F32, name="warm")
@@ -329,45 +359,24 @@ def tile_pseudohuberphylogeneticcontrastcrossmome_x1_kernel(
             cut_ps = t_bank()
             nc.tensor.transpose(cut_ps[:, 0:128], rows32[:], ident[:])
             nc.vector.reciprocal(out=icut[:], in_=cut_ps[:, 0:16])
-            interleave(("y", 0, 0), 0, 256, Y0[0])
-            interleave(("y", 0, 1), 0, 256, Y0[1])
-            yz_quant(("y", 0, 0), 0, 256)
-            yz_quant(("y", 0, 1), 0, 256)
-
-            side = {}
-
-            def add_side(step, job):
-                side.setdefault(step, []).append(job)
-
             l_banks = {}
 
-            def l_turn(tp):
-                for h in range(2):
-                    l_banks[tp, h] = o_bank()
-                    l_transpose(1, h, tp, l_banks[tp, h])
-
-            def l_out(tp):
-                l_copy(1, 0, tp, l_banks[tp, 0], L1[2 * tp])
-                l_copy(1, 1, tp, l_banks[tp, 1], L1[2 * tp + 1])
-
-            def half(key, lo, engine):
-                def run():
-                    piece = PIECE if engine == "pool" else 256
-                    for at in range(lo, lo + 256, piece):
-                        interleave(key, at, at + piece, engine)
-
-                return run
-
-            def quant_job(key):
-                return lambda: yz_quant(key)
-
-            add_side(0, lambda: l_quant(1, 0))
-            add_side(0, lambda: l_quant(1, 1))
-            for which, c, plan, first, at in (("y", 1, Y1, YSTEP, YQ), ("z", 0, Z0, Z0STEP, Z0Q), ("z", 1, Z1, Z1STEP, Z1Q)):
-                for m in range(4):
-                    add_side(first + (m if plan[m] != "pool" else 0), half((which, c, m // 2), 256 * (m % 2), plan[m]))
-                for h in range(2):
-                    add_side(at[h], quant_job((which, c, h)))
+            def run_side(job):
+                kind = job[1]
+                if kind == "copy":
+                    piece = PIECE if job[6] == "pool" else 256
+                    for lo in range(job[5], job[5] + 256, piece):
+                        interleave((job[2], job[3], job[4]), lo, lo + piece, job[6])
+                elif kind == "quant":
+                    yz_quant((job[2], job[3], job[4]), job[5], job[6])
+                elif kind == "turn":
+                    for h in range(2):
+                        l_banks[job[2], h] = o_bank()
+                        l_transpose(1, h, job[2], l_banks[job[2], h])
+                elif kind == "lout":
+                    l_copy(1, job[3], job[2], l_banks[job[2], job[3]], job[4])
+                elif kind == "lquant":
+                    l_quant(1, job[2])
 
             last_of = {}
             for i, (which, tile, g) in enumerate(units):
@@ -379,37 +388,23 @@ def tile_pseudohuberphylogeneticcontrastcrossmome_x1_kernel(
             groups = []
             quants = []
             n = len(units)
-            mm(0)
-            mm(1)
-            interleave(("y", 0, 0), 256, 512, Y0[2])
-            interleave(("y", 0, 1), 256, 512, Y0[3])
-            yz_quant(("y", 0, 0), 256, 512)
-            yz_quant(("y", 0, 1), 256, 512)
-            square(0)
-            l_turn(0)
-            mm(2)
-            square(1)
-            rsqrt(0)
-            l_turn(1)
-            l_out(0)
-            l_out(1)
-            i = 0
+            i = -1 - MA
             done = 0
             copied = 0
             while i < n + LAG or jobs or copies or groups or quants:
-                if i + AHEAD < n:
-                    mm(i + AHEAD)
+                if 0 <= i + MA < n:
+                    mm(i + MA)
                 new_copy = []
-                for unused in range(1 if i < n + LAG else 2):
+                for unused in range(EARLYJ if i < n + LAG - 1 else TAILJ):
                     if jobs:
                         job = jobs.pop(0)
                         out_mm(job)
                         new_copy.append(job)
-                if i + 2 < n:
+                if 0 <= i + 2 < n:
                     square(i + 2)
-                if i + 1 < n:
+                if 0 <= i + 1 < n:
                     rsqrt(i + 1)
-                if i < n:
+                if 0 <= i < n:
                     product(i)
                     turn(i)
                 if LAG <= i < n + LAG:
@@ -421,14 +416,19 @@ def tile_pseudohuberphylogeneticcontrastcrossmome_x1_kernel(
                 if len(quants) > (1 if groups or copies or i < n else 0):
                     out_quant(*quants.pop(0))
                 for m, job in enumerate(copies):
+                    direct = job[3] == 4 and OG[2 * job[0] + job[1]] == "psum"
+                    if direct:
+                        out_group(job[0], job[1], "psum")
+                        quants.append((job[0], job[1]))
                     out_copy(job, OUT[copied])
                     copied += 1
-                    if job[2] + job[3] == 4:
+                    if job[2] + job[3] == 4 and not direct:
                         groups.append((job[0], job[1]))
                 copies = new_copy
-                for job in side.get(i, []):
-                    job()
-                while done < (i - LAG if i < n else i - LAG + 1):
+                for job in SIDE:
+                    if job[0] == i:
+                        run_side(job)
+                while done < (i - LAG + 1 - QLAG if i < n else i - LAG + 1):
                     key = key_after.get(done)
                     done += 1
                     if key is not None:

from contextlib import ExitStack

import concourse.mybir as mybir
from concourse.masks import make_identity

F32 = mybir.dt.float32
BF16 = mybir.dt.bfloat16
U32 = mybir.dt.uint32
I32 = mybir.dt.int32
U8 = mybir.dt.uint8
FP8X4 = mybir.dt.float8_e4m3fn_x4
ACTF = mybir.ActivationFunctionType
ALU = mybir.AluOpType

N = 1024
P = 128
FLOPS = 3 * 2 * N * N * N

CHUNKS = ((0, 256), (256, 256), (512, 256), (768, 256))
PIECE = 128
LAG = 1
UORD = 'cg'
UB = 4
MA = 3
TAILJ = 2
EARLYJ = 1
QLAG = 1
L0 = ('dve', 'act', 'act', 'dve')
OG = ('pool', 'pool', 'pool', 'pool', 'act', 'dve', 'dve', 'dve', 'dve', 'dve', 'dve', 'dve')
OUT = ('act',) * 11 + ('dve',) + ('act',) * 2 + ('dve',) + ('act',) * 5
SIDE = ((-4, 'copy', 'y', 0, 0, 0, 'act'), (-4, 'copy', 'y', 0, 1, 0, 'act'), (-4, 'copy', 'y', 0, 1, 256, 'pool'), (-4, 'quant', 'y', 0, 0, 0, 256), (-4, 'quant', 'y', 0, 1, 0, 256), (-4, 'turn', 0), (-3, 'copy', 'y', 0, 0, 256, 'act'), (-3, 'quant', 'y', 0, 1, 256, 512), (-3, 'copy', 'y', 1, 0, 0, 'pool'), (-2, 'quant', 'y', 0, 0, 256, 512), (-2, 'turn', 1), (-2, 'copy', 'y', 1, 0, 256, 'pool'), (-2, 'lout', 0, 0, 'dve'), (-1, 'lout', 1, 0, 'dve'), (-1, 'lout', 1, 1, 'dve'), (-1, 'lout', 0, 1, 'act'), (-1, 'lquant', 0), (-1, 'copy', 'y', 1, 1, 0, 'pool'), (0, 'lquant', 1), (1, 'copy', 'y', 1, 1, 256, 'pool'), (2, 'copy', 'z', 0, 0, 0, 'pool'), (2, 'quant', 'y', 1, 0, 0, 512), (4, 'quant', 'y', 1, 1, 0, 512), (5, 'copy', 'z', 0, 0, 256, 'pool'), (7, 'copy', 'z', 0, 1, 0, 'pool'), (7, 'quant', 'z', 0, 0, 0, 512), (8, 'copy', 'z', 0, 1, 256, 'pool'), (9, 'copy', 'z', 1, 0, 0, 'pool'), (9, 'copy', 'z', 1, 0, 256, 'act'), (10, 'quant', 'z', 0, 1, 0, 512), (12, 'quant', 'z', 1, 0, 0, 512), (13, 'copy', 'z', 1, 1, 0, 'pool'), (14, 'copy', 'z', 1, 1, 256, 'act'), (15, 'quant', 'z', 1, 1, 0, 512))


def tile_pseudohuberphylogeneticcontrastcrossmome_x1_kernel(
    tc, l, y, z, cy, cz, g1, g2, out_0, out_1, out_2
):
    nc = tc.nc
    with ExitStack() as ctx:
        keep = ctx.enter_context(tc.tile_pool(name="keep", bufs=1))
        work = ctx.enter_context(tc.tile_pool(name="work", bufs=3))
        psum = ctx.enter_context(tc.psum_pool(name="psum", bufs=1))

        def u_bank():
            return psum.tile([P, 512], F32, name="u_ps", tag="u_ps", bufs=UB)

        def t_bank():
            return psum.tile([P, 512], F32, name="t_ps", tag="to_ps", bufs=8 - UB)

        def o_bank():
            return psum.tile([P, 512], F32, name="o_ps", tag="to_ps", bufs=8 - UB)

        rows = keep.tile([P, P], BF16, name="rows")
        nc.vector.memset(rows[:], 0.0)
        l_raw = {}
        l_view = l.rearrange("(g m t) s -> g m t s", g=2, t=4)

        def load_l(g):
            if g == 0:
                for t in range(4):
                    tile = keep.tile([P, N], BF16, name="l_raw_0_%d" % t)
                    nc.sync.dma_start(out=tile[:], in_=l_view[g][:, t, :])
                    l_raw[g, t] = tile[:]
            else:
                for tp in range(2):
                    tile = keep.tile([P, 2, N], BF16, name="l_raw_1_%d" % tp)
                    nc.sync.dma_start(out=tile[:], in_=l_view[g][:, 2 * tp : 2 * tp + 2, :])
                    l_raw[g, 2 * tp] = tile[:, 0, :]
                    l_raw[g, 2 * tp + 1] = tile[:, 1, :]

        raw = {}
        views = {"y": y.rearrange("(h p j) w -> h p j w", h=2, j=4), "z": z.rearrange("(h p j) w -> h p j w", h=2, j=4)}

        def load_yz(which, c):
            width = 256 if (which, c) == ("y", 0) else 512
            for lo in range(0, 512, width):
                for h in range(2):
                    tile = keep.tile([P, 4, width], BF16, name="raw_%s_%d_%d_%d" % (which, c, h, lo))
                    nc.sync.dma_start(out=tile[:], in_=views[which][h][:, :, 512 * c + lo : 512 * c + lo + width])
                    for at in range(lo, lo + width, 128):
                        raw[which, c, h, at] = (tile, at - lo)

        load_l(0)
        nc.scalar.dma_start(out=rows[0:8, :], in_=cy.rearrange("(i n) -> i n", n=P))
        nc.scalar.dma_start(out=rows[8:16, :], in_=cz.rearrange("(i n) -> i n", n=P))
        gain = []
        for name, src in (("g1", g1), ("g2", g2)):
            gt = keep.tile([P, 2, 4], BF16, name="gain_" + name)
            nc.scalar.dma_start(out=gt[:], in_=src.rearrange("(g p t) -> p g t", g=2, t=4))
            gain.append(gt)
        load_yz("y", 0)
        if UORD == "gc":
            load_yz("y", 1)
            load_l(1)
        else:
            load_l(1)
            load_yz("y", 1)
        load_yz("z", 0)
        load_yz("z", 1)

        ident = keep.tile([P, P], F32, name="ident")
        make_identity(nc, ident[:])

        l_grp = [[keep.tile([P, 512, 4], BF16, name="l_grp_%d_%d" % (g, h), align_bytes=64) for h in range(2)] for g in range(2)]
        l_codes = [[keep.tile([P, 512], U32, name="l_codes_%d_%d" % (g, h), align_bytes=64) for h in range(2)] for g in range(2)]
        l_scales = [[keep.tile([P, 512], U8, name="l_scales_%d_%d" % (g, h), align_bytes=64) for h in range(2)] for g in range(2)]

        def l_transpose(g, h, tp, bank, slots=(0, 1)):
            for tt in slots:
                words = l_raw[g, 2 * tp + tt].bitcast(F32)
                for u in range(2):
                    nc.tensor.transpose(
                        bank[:, 256 * u + 128 * tt : 256 * u + 128 * tt + 128],
                        words[:, 256 * h + u : 256 * h + 256 : 2],
                        ident[:],
                    )

        def l_copy(g, h, tp, bank, engine):
            dst = l_grp[g][h][:, 256 * tp : 256 * tp + 256, :].rearrange("p r j -> p (r j)").bitcast(F32)
            src = bank[:].rearrange("p (u r) -> p r u", u=2)
            dst = dst.rearrange("p (r u) -> p r u", u=2)
            if engine == "act":
                nc.scalar.copy(out=dst, in_=src)
            else:
                nc.vector.tensor_copy(out=dst, in_=src)

        def quantize(codes, scales, grp):
            nc.vector.quantize_mx(out=codes.bitcast(FP8X4), scales=scales, in_=grp)

        def l_quant(g, h, lo=0, hi=512):
            quantize(l_codes[g][h][:, lo:hi], l_scales[g][h][:, lo:hi], l_grp[g][h][:, lo:hi, :].rearrange("p r j -> p (r j)"))

        grp = {}
        codes = {}
        scales = {}

        def interleave(key, lo, hi, engine):
            if key not in grp:
                grp[key] = keep.tile([P, 512, 4], BF16, name="grp_%s_%d_%d" % key, align_bytes=64)
            dst = grp[key][:, lo:hi, :]
            tile, at = raw[key[0], key[1], key[2], lo]
            src = tile[:, :, at : at + hi - lo]
            if engine == "pool":
                src = src.rearrange("p j w -> p w j")
            else:
                src = src.rearrange("p j (w i) -> p w j i", i=4)
                dst = dst.rearrange("p (w i) j -> p w j i", i=4)
            if engine == "act":
                nc.scalar.copy(out=dst, in_=src)
            elif engine == "pool":
                nc.gpsimd.tensor_scalar(out=dst, in0=src, scalar1=1.0, scalar2=0.0, op0=ALU.mult, op1=ALU.add)
            else:
                nc.vector.tensor_copy(out=dst, in_=src)

        def yz_quant(key, lo=0, hi=512):
            if key not in codes:
                codes[key] = keep.tile([P, 512], U32, name="codes_%s_%d_%d" % key, align_bytes=64)
                scales[key] = keep.tile([P, 512], U8, name="scales_%s_%d_%d" % key, align_bytes=64)
            quantize(codes[key][:, lo:hi], scales[key][:, lo:hi], grp[key][:, lo:hi, :].rearrange("p w j -> p (w j)"))

        icut = keep.tile([P, 16], F32, name="icut")

        units = []
        for first in range(2):
            for second in range(2):
                c, g = (first, second) if UORD == "cg" else (second, first)
                for ii in range(4):
                    units.append(("y", 4 * c + ii, g))
        chunk_of = {}
        for k, (lo, width) in enumerate(CHUNKS):
            for g in range(2):
                for tile in range(lo // 128, (lo + width) // 128):
                    units.append(("z", tile, g))
                    chunk_of[tile] = k

        u_ps = {}
        sq = {}
        rs = {}
        prod = {}
        t_ps = {}

        def mm(i):
            which, tile, g = units[i]
            u_ps[i] = u_bank()
            c, lo = tile // 4, 128 * (tile % 4)
            for h in range(2):
                nc.tensor.matmul_mx(
                    out=u_ps[i][:],
                    lhsT=codes[which, c, h][:, lo : lo + 128].bitcast(FP8X4),
                    lhsT_scale=scales[which, c, h][:, lo : lo + 128],
                    rhs=l_codes[g][h][:].bitcast(FP8X4),
                    rhs_scale=l_scales[g][h][:],
                    start=(h == 0),
                    stop=(h == 1),
                )

        def square(i):
            which, tile, g = units[i]
            col = tile + (8 if which == "z" else 0)
            sq[i] = work.tile([P, 512], F32, name="sq", bufs=4)
            nc.scalar.activation(out=sq[i][:], in_=u_ps[i][:], func=ACTF.Square, scale=icut[:, col : col + 1])

        def rsqrt(i):
            rs[i] = work.tile([P, 512], F32, name="rs", bufs=4)
            nc.scalar.activation(out=rs[i][:], in_=sq[i][:], func=ACTF.Abs_reciprocal_sqrt, bias=1.0, scale=1.0)

        def product(i):
            prod[i] = work.tile([P, 512], F32, name="prod", bufs=3)
            nc.vector.tensor_tensor(out=prod[i][:], in0=u_ps[i][:], in1=rs[i][:], op=ALU.mult)

        def turn(i):
            t_ps[i] = t_bank()
            for t in range(4):
                nc.tensor.transpose(t_ps[i][:, 128 * t : 128 * t + 128], prod[i][:, 128 * t : 128 * t + 128], ident[:])

        ab_grp = {}
        ab_codes = {}
        ab_scales = {}
        for which in "yz":
            for g in range(2):
                ab_codes[which, g] = keep.tile([P, N], U32, name="ab_codes_%s_%d" % (which, g), align_bytes=64)
                ab_scales[which, g] = keep.tile([P, N], U8, name="ab_scales_%s_%d" % (which, g), align_bytes=64)

        def weigh(i):
            which, tile, g = units[i]
            if which == "y":
                c, ii = tile // 4, tile % 4
                key = (which, c, g)
                if key not in ab_grp:
                    ab_grp[key] = work.tile([P, 512, 4], BF16, name="a_grp", bufs=2, align_bytes=64)
                dst = ab_grp[key][:].rearrange("p (t m) j -> p t m j", t=4)[:, :, 32 * ii : 32 * ii + 32, :]
                src = t_ps[i][:].rearrange("k (j m t) -> k t m j", j=4, t=4)
                fac = gain[0][:, g, :].unsqueeze(1).unsqueeze(1).to_broadcast([P, 4, 32, 4])
            else:
                k = chunk_of[tile]
                ii = tile - CHUNKS[k][0] // 128
                key = (which, k, g)
                if key not in ab_grp:
                    ab_grp[key] = work.tile([P, 256, 4], BF16, name="b_grp", bufs=3, align_bytes=64)
                dst = ab_grp[key][:, 128 * ii : 128 * ii + 128, :]
                src = t_ps[i][:].rearrange("k (j n) -> k n j", j=4)
                fac = gain[1][:, g, :].unsqueeze(1).to_broadcast([P, 128, 4])
            nc.vector.tensor_tensor(out=dst, in0=src, in1=fac, op=ALU.mult)

        def ab_quant(key):
            which, c, g = key
            lo, width = (512 * c, 512) if which == "y" else CHUNKS[c]
            cols = slice(lo, lo + width)
            quantize(
                ab_codes[which, g][:, cols], ab_scales[which, g][:, cols], ab_grp[key][:, 0:width, :].rearrange("p w j -> p (w j)")
            )

        o_ps = {}
        of = {}
        og = {}
        w_codes = {}

        def out_mm(job):
            k, big, first, count = job
            lo, width = CHUNKS[k]
            o_ps[job] = o_bank()
            for tt in range(count):
                row = 512 * big + 128 * (first + tt)
                for g in range(2):
                    nc.tensor.matmul_mx(
                        out=o_ps[job][:, width * tt : width * tt + width],
                        lhsT=ab_codes["y", g][:, row : row + 128].bitcast(FP8X4),
                        lhsT_scale=ab_scales["y", g][:, row : row + 128],
                        rhs=ab_codes["z", g][:, lo : lo + width].bitcast(FP8X4),
                        rhs_scale=ab_scales["z", g][:, lo : lo + width],
                        start=(g == 0),
                        stop=(g == 1),
                    )

        def out_copy(job, engine):
            k, big, first, count = job
            lo, width = CHUNKS[k]
            if first == 0:
                of[k, big] = work.tile([P, 4, 256], F32, name="of", bufs=6)
            dst = of[k, big][:, first : first + count, 0:width]
            src = o_ps[job][:].rearrange("p (t m) -> p t m", t=count)
            if engine == "act":
                nc.scalar.activation(out=dst, in_=src, func=ACTF.Copy, scale=1.0 / 32.0)
            else:
                nc.vector.tensor_scalar(out=dst, in0=src, scalar1=1.0 / 32.0, scalar2=None, op0=ALU.mult)
            if first + count == 4:
                nc.sync.dma_start(
                    out=out_0[512 * big : 512 * big + 512, lo : lo + width].rearrange("(p t) m -> p t m", t=4),
                    in_=of[k, big][:, :, 0:width],
                )

        def out_group(k, big, engine):
            width = CHUNKS[k][1]
            og[k, big] = work.tile([P, 256, 4], BF16, name="og", bufs=4, align_bytes=64)
            dst = og[k, big][:, 0:width, :]
            if engine == "psum":
                src = o_ps[k, big, 0, 4][:].rearrange("p (t m) -> p m t", t=4)
                nc.vector.tensor_scalar(out=dst, in0=src, scalar1=1.0 / 32.0, scalar2=None, op0=ALU.mult)
                return
            src = of[k, big][:, :, 0:width]
            if engine == "pool":
                src = src.rearrange("p t m -> p m t")
                for lo in range(0, width, PIECE):
                    nc.gpsimd.tensor_scalar(
                        out=dst[:, lo : lo + PIECE, :], in0=src[:, lo : lo + PIECE, :], scalar1=1.0, scalar2=0.0, op0=ALU.mult, op1=ALU.add
                    )
                return
            else:
                src = src.rearrange("p t (m i) -> p m t i", i=4)
                dst = dst.rearrange("p (m i) t -> p m t i", i=4)
            if engine == "pool":
                nc.gpsimd.tensor_scalar(out=dst, in0=src, scalar1=1.0, scalar2=0.0, op0=ALU.mult, op1=ALU.add)
            elif engine == "act":
                nc.scalar.copy(out=dst, in_=src)
            else:
                nc.vector.tensor_copy(out=dst, in_=src)

        w_scales = [keep.tile([P, 2, 512], U8, name="w_scales_%d" % half, align_bytes=64) for half in range(2)]

        def out_quant(k, big):
            lo, width = CHUNKS[k]
            if big == 0:
                w_codes[k] = work.tile([P, 2, 256], U32, name="w_codes", bufs=4, align_bytes=64)
            plane = w_scales[lo // 512]
            quantize(
                w_codes[k][:, big, 0:width],
                plane[:, big, lo % 512 : lo % 512 + width],
                og[k, big][:, 0:width, :].rearrange("p m t -> p (m t)"),
            )
            if big == 1:
                nc.sync.dma_start(
                    out=out_1[:, :, lo : lo + width, :].rearrange("g p m t -> p g (m t)").bitcast(I32),
                    in_=w_codes[k][:, :, 0:width].bitcast(I32),
                )
                if (lo + width) % 512 == 0:
                    half = lo // 512
                    for q in range(4):
                        nc.sync.dma_start(
                            out=out_2[:, 4 * q : 4 * q + 4, 512 * half : 512 * half + 512].rearrange("g r m -> r g m").bitcast(I32),
                            in_=plane[32 * q : 32 * q + 4, :, :].bitcast(I32),
                        )

        with tc.manual_schedule(engines={mybir.EngineType.PE, mybir.EngineType.Activation, mybir.EngineType.DVE}):
            warm = keep.tile([P, 1], F32, name="warm")
            nc.vector.memset(warm[:], 1.0)
            nc.scalar.activation(out=warm[:], in_=warm[:], func=ACTF.Abs_reciprocal_sqrt, bias=1.0, scale=1.0)

            for tp in range(2):
                banks = [u_bank(), u_bank()]
                for tt in range(2):
                    for h in range(2):
                        l_transpose(0, h, tp, banks[h], (tt,))
                for h in range(2):
                    l_copy(0, h, tp, banks[h], L0[2 * tp + h])
                if tp == 0:
                    rows32 = keep.tile([P, P], F32, name="rows32")
                    nc.vector.tensor_copy(out=rows32[:], in_=rows[:])
                for h in range(2):
                    l_quant(0, h, 256 * tp, 256 * tp + 256)
            cut_ps = t_bank()
            nc.tensor.transpose(cut_ps[:, 0:128], rows32[:], ident[:])
            nc.vector.reciprocal(out=icut[:], in_=cut_ps[:, 0:16])
            l_banks = {}

            def run_side(job):
                kind = job[1]
                if kind == "copy":
                    piece = PIECE if job[6] == "pool" else 256
                    for lo in range(job[5], job[5] + 256, piece):
                        interleave((job[2], job[3], job[4]), lo, lo + piece, job[6])
                elif kind == "quant":
                    yz_quant((job[2], job[3], job[4]), job[5], job[6])
                elif kind == "turn":
                    for h in range(2):
                        l_banks[job[2], h] = o_bank()
                        l_transpose(1, h, job[2], l_banks[job[2], h])
                elif kind == "lout":
                    l_copy(1, job[3], job[2], l_banks[job[2], job[3]], job[4])
                elif kind == "lquant":
                    l_quant(1, job[2])

            last_of = {}
            for i, (which, tile, g) in enumerate(units):
                last_of[which, tile // 4 if which == "y" else chunk_of[tile], g] = i
            key_after = {i: key for key, i in last_of.items()}

            jobs = []
            copies = []
            groups = []
            quants = []
            n = len(units)
            i = -1 - MA
            done = 0
            copied = 0
            while i < n + LAG or jobs or copies or groups or quants:
                if 0 <= i + MA < n:
                    mm(i + MA)
                new_copy = []
                for unused in range(EARLYJ if i < n + LAG - 1 else TAILJ):
                    if jobs:
                        job = jobs.pop(0)
                        out_mm(job)
                        new_copy.append(job)
                if 0 <= i + 2 < n:
                    square(i + 2)
                if 0 <= i + 1 < n:
                    rsqrt(i + 1)
                if 0 <= i < n:
                    product(i)
                    turn(i)
                if LAG <= i < n + LAG:
                    weigh(i - LAG)
                if groups:
                    grp_key = groups.pop(0)
                    out_group(grp_key[0], grp_key[1], OG[2 * grp_key[0] + grp_key[1]])
                    quants.append(grp_key)
                if len(quants) > (1 if groups or copies or i < n else 0):
                    out_quant(*quants.pop(0))
                for m, job in enumerate(copies):
                    direct = job[3] == 4 and OG[2 * job[0] + job[1]] == "psum"
                    if direct:
                        out_group(job[0], job[1], "psum")
                        quants.append((job[0], job[1]))
                    out_copy(job, OUT[copied])
                    copied += 1
                    if job[2] + job[3] == 4 and not direct:
                        groups.append((job[0], job[1]))
                copies = new_copy
                for job in SIDE:
                    if job[0] == i:
                        run_side(job)
                while done < (i - LAG + 1 - QLAG if i < n else i - LAG + 1):
                    key = key_after.get(done)
                    done += 1
                    if key is not None:
                        ab_quant(key)
                        if key[0] == "z" and key[2] == 1:
                            count = 512 // CHUNKS[key[1]][1]
                            jobs.extend((key[1], big, first, count) for big in range(2) for first in range(0, 4, count))
                i += 1
